import numpy as np
import ml_dtypes


def mxq(x, axis, fmt="e4m3"):
    dtype, down = {"e4m3": (ml_dtypes.float8_e4m3fn, 7), "e5m2": (ml_dtypes.float8_e5m2, 14)}[fmt]
    v = np.moveaxis(np.asarray(x, np.float32).astype(ml_dtypes.bfloat16).astype(np.float64), axis, -1)
    blocks = v.reshape(v.shape[:-1] + (-1, 32))
    amax = np.abs(blocks).max(-1, keepdims=True)
    byte = np.maximum(np.where(amax > 0, np.frexp(amax)[1] - 1 + 127, 0) - down, 1)
    scale = np.exp2(byte - 127.0)
    codes = (blocks / scale).astype(np.float32).astype(dtype).astype(np.float64)
    return np.moveaxis((codes * scale).reshape(v.shape), -1, axis)


WIDE = False


def mx_kscale(k):
    if not WIDE:
        return np.ones(k)
    levels = np.array([10, -10, 5, -5, 0])
    if k % 512:
        return np.exp2(np.random.permutation(np.resize(levels, k // 32))).repeat(32)
    a = np.empty((k // 512, 16))
    for p in range(k // 512):
        a[p, :8] = np.random.permutation(np.resize(levels, 8))
        for g in range(8):
            far = levels[np.abs(levels - a[p, g]) >= 10]
            a[p, g + 8] = far[np.random.randint(len(far))]
    return np.exp2(a.ravel()).repeat(32)


def f64(x):
    return np.asarray(x).astype(np.float64)


def striped(idx):
    return np.tile(idx.reshape(-1, 16).T, (8, 1)).astype(np.uint16)


def unstriped(offs):
    return offs[:16].T.reshape(-1).astype(np.int64)


E2M1 = np.array([0.0, 0.5, 1.0, 1.5, 2.0, 3.0, 4.0, 6.0, -0.0, -0.5, -1.0, -1.5, -2.0, -3.0, -4.0, -6.0])


def pack_weight(w, fmt):
    k, n = w.shape
    w = f64(np.asarray(w, np.float32).astype(ml_dtypes.bfloat16)).reshape(k // 32, 32, n)
    amax = np.abs(w).max(1)
    if fmt == "e4m3":
        byte = np.frexp(amax)[1] - 1 + 127 - 7
    else:
        mant, ex = np.frexp(amax / 6.0)
        byte = np.where(mant > 0.5, ex, ex - 1) + 127
    byte = np.clip(np.where(amax > 0, byte, 1), 1, 254)
    scaled = (w * np.exp2(127.0 - byte)[:, None, :]).reshape(k, n).astype(np.float32)
    by_word = np.ascontiguousarray(scaled.reshape(k // 512, 128, 4, n).transpose(0, 1, 3, 2))
    if fmt == "e4m3":
        words = by_word.astype(ml_dtypes.float8_e4m3fn).view(np.uint8)
    else:
        c = by_word.astype(ml_dtypes.float4_e2m1fn).view(np.uint8) & 0xF
        words = (c[..., 0::2] | (c[..., 1::2] << 4)).reshape(k // 512, 128, 2 * n)
    return np.ascontiguousarray(words), np.ascontiguousarray(byte.astype(np.uint8).reshape(k // 512, 16, n))


def unpack_weight(words, scales, fmt):
    g, _, n = scales.shape
    words = np.ascontiguousarray(words).reshape(g, 128, n, -1)
    if fmt == "e4m3":
        vals = words.view(ml_dtypes.float8_e4m3fn).astype(np.float64)
    else:
        nib = np.empty((g, 128, n, 4), np.uint8)
        nib[..., 0::2] = words & 0xF
        nib[..., 1::2] = words >> 4
        vals = E2M1[nib]
    vals = vals * np.repeat(np.exp2(scales.astype(np.float64) - 127.0), 8, axis=1)[..., None]
    return vals.transpose(0, 1, 3, 2).reshape(g * 512, n)


def gelu(v):
    return 0.5 * v * (1.0 + np.tanh(np.sqrt(2.0 / np.pi) * (v + 0.044715 * v**3)))


K, M, T, S = 512, 256, 4096, 1536


def setup_inputs():
    n = np.random.standard_normal
    s = mx_kscale(K)[:, None]
    s2 = mx_kscale(512)[:, None]
    v = pack_weight(n((K, T)) * s, "e4m3")
    p_w4 = pack_weight(n((K, M)) / np.sqrt(K) / s, "e2m1")
    return {
        "tab_words": v[0],
        "tab_scales": v[1],
        "w4_words": p_w4[0],
        "w4_scales": p_w4[1],
        "c": (n((512, S)) * s2).astype(np.float32),
        "u": (n((512, M)) / np.sqrt(512) / s2).astype(np.float32),
        "rT": n((M, T)).astype(np.float32),
        "b": (0.3 * n(256)).astype(np.float32),
        "offs": striped(np.random.permutation(T)[:S]),
    }


def reference(tab_words, tab_scales, w4_words, w4_scales, c, u, rT, b, offs):
    tab_ = unpack_weight(tab_words, tab_scales, "e4m3")[:, unstriped(offs)]
    w4_ = unpack_weight(w4_words, w4_scales, "e2m1")
    c_ = mxq(f64(c), 0, "e4m3")
    u_ = mxq(f64(u), 0, "e4m3")
    y = w4_.T @ tab_ + u_.T @ c_
    return (gelu(y + f64(b)[:, None])) + f64(rT)[:, unstriped(offs)]

@@ -1,0 +1,163 @@
+from contextlib import ExitStack
+
+import concourse.mybir as mybir
+
+K, M, T, S = 512, 256, 4096, 1536
+FLOPS = 2 * 2 * K * M * S
+
+F32 = mybir.dt.float32
+BF16 = mybir.dt.bfloat16
+I32 = mybir.dt.int32
+U32 = mybir.dt.uint32
+U16 = mybir.dt.uint16
+U8 = mybir.dt.uint8
+FP8X4 = mybir.dt.float8_e4m3fn_x4
+FP4X4 = mybir.dt.float4_e2m1fn_x4
+GELU = mybir.ActivationFunctionType.Gelu_apprx_tanh
+ADD = mybir.AluOpType.add
+
+P = 128
+PACK = 4
+HALVES = M // P
+BANK = 512
+PIECE = 256
+VECTOR_PIECES = (3, 5)
+
+
+def interleave(copy, grouped, raw):
+    copy(
+        grouped.rearrange("p (c i t) -> p c t i", i=2, t=PACK),
+        raw.rearrange("p t (c i) -> p c t i", i=2),
+    )
+
+
+def tile_list_tabres_gelu_kernel(
+    tc, tab_words, tab_scales, w4_words, w4_scales, c, u, rT, b, offs, out
+):
+    nc = tc.nc
+    with ExitStack() as ctx:
+        keep = ctx.enter_context(tc.tile_pool(name="keep", bufs=1))
+        psum = ctx.enter_context(tc.psum_pool(name="psum", bufs=1))
+
+        offsets = keep.tile([P, S // 16], U16, name="offsets")
+        nc.sync.dma_start(offsets[:], offs)
+
+        table_scales = keep.tile([P, T // 4], I32, name="table_scales")
+        nc.vector.memset(table_scales[:], 0)
+        w4_plane = keep.tile([P, M // 4], I32, name="w4_plane", align_bytes=64)
+        nc.vector.memset(w4_plane[:], 0)
+        for q in range(4):
+            nc.gpsimd.dma_start(table_scales[32 * q : 32 * q + 4, :], tab_scales[0, 4 * q : 4 * q + 4, :].bitcast(I32))
+        for q in range(4):
+            nc.gpsimd.dma_start(w4_plane[32 * q : 32 * q + 4, :], w4_scales[0, 4 * q : 4 * q + 4, :].bitcast(I32))
+
+        table_words = keep.tile([P, T], I32, name="table_words")
+        nc.sync.dma_start(table_words[:], tab_words[0].rearrange("p t i -> p (t i)").bitcast(I32))
+
+        bias = keep.tile([P, HALVES], F32, name="bias")
+        with nc.allow_non_contiguous_dma(reason="one bias value a partition"):
+            nc.scalar.dma_start(bias[:], b.rearrange("(h p) -> p h", p=P))
+        w4_codes = keep.tile([P, 2 * M], U8, name="w4_codes", align_bytes=64)
+        nc.scalar.dma_start(w4_codes[:].bitcast(I32), w4_words[0].bitcast(I32))
+        warm = keep.tile([P, 1], F32, name="warm")
+        nc.scalar.activation(warm[:], bias[:, 0:1], GELU)
+
+        residual = []
+        for h in range(HALVES):
+            window = keep.tile([P, T], F32, name="residual%d" % h)
+            nc.sync.dma_start(window[:], rT[h * P : (h + 1) * P, :])
+            residual.append(window)
+        u_raw = keep.tile([P, PACK, M], F32, name="u_raw")
+        nc.sync.dma_start(u_raw[:], u.rearrange("(p t) n -> p t n", t=PACK))
+        c_rows = c.rearrange("(p t) j -> p t j", t=PACK)
+        c_raw = []
+        for i in range(S // PIECE):
+            raw = keep.tile([P, PACK, PIECE], F32, name="c_raw%d" % i)
+            nc.sync.dma_start(raw[:], c_rows[:, :, i * PIECE : (i + 1) * PIECE])
+            c_raw.append(raw)
+
+        picked_scales = keep.tile([P, S], U8, name="picked_scales", align_bytes=64)
+        nc.vector.tensor_copy(picked_scales[:], table_scales[:].bitcast(U8).indirect(offsets[:]))
+        picked_words = keep.tile([P, S], U32, name="picked_words", align_bytes=64)
+        nc.vector.tensor_copy(picked_words[:], table_words[:].bitcast(U32).indirect(offsets[:]))
+        picked_residual = []
+        for h in range(HALVES):
+            picked = keep.tile([P, S], F32, name="picked_residual%d" % h)
+            nc.vector.tensor_copy(picked[:], residual[h][:].indirect(offsets[:]))
+            picked_residual.append(picked)
+
+        sums = {}
+        for g in range(S // BANK):
+            for h in range(HALVES):
+                cols = slice(g * BANK, (g + 1) * BANK)
+                sums[g, h] = psum.tile([P, BANK], F32, name="sum%d_%d" % (g, h))
+                nc.tensor.matmul_mx(
+                    out=sums[g, h][:],
+                    lhsT=w4_codes[:, 2 * h * P : 2 * (h + 1) * P].bitcast(FP4X4),
+                    lhsT_scale=w4_plane[:].bitcast(U8)[:, h * P : (h + 1) * P],
+                    rhs=picked_words[:, cols].bitcast(FP8X4),
+                    rhs_scale=picked_scales[:, cols],
+                    start=True,
+                    stop=False,
+                )
+
+        u_grouped = keep.tile([P, PACK * M], BF16, name="u_grouped", align_bytes=64)
+        interleave(nc.scalar.copy, u_grouped[:], u_raw[:])
+        u_codes = keep.tile([P, M], U32, name="u_codes", align_bytes=64)
+        u_plane = keep.tile([P, M], U8, name="u_plane", align_bytes=64)
+        nc.vector.quantize_mx(out=u_codes[:].bitcast(FP8X4), scales=u_plane[:], in_=u_grouped[:])
+
+        grouped = {}
+        activated = {}
+
+        def round_piece(i):
+            grouped[i] = keep.tile([P, PACK * PIECE], BF16, name="c_grouped%d" % i, align_bytes=64)
+            copy = nc.vector.tensor_copy if i in VECTOR_PIECES else nc.scalar.copy
+            interleave(copy, grouped[i][:], c_raw[i][:])
+
+        def multiply_piece(i):
+            codes = keep.tile([P, PIECE], U32, name="c_codes%d" % i, align_bytes=64)
+            plane = keep.tile([P, PIECE], U8, name="c_plane%d" % i, align_bytes=64)
+            nc.vector.quantize_mx(out=codes[:].bitcast(FP8X4), scales=plane[:], in_=grouped[i][:])
+            g, part = divmod(i, BANK // PIECE)
+            for h in range(HALVES):
+                nc.tensor.matmul_mx(
+                    out=sums[g, h][:, part * PIECE : (part + 1) * PIECE],
+                    lhsT=u_codes[:, h * P : (h + 1) * P].bitcast(FP8X4),
+                    lhsT_scale=u_plane[:, h * P : (h + 1) * P],
+                    rhs=codes[:].bitcast(FP8X4),
+                    rhs_scale=plane[:],
+                    start=False,
+                    stop=(part == BANK // PIECE - 1),
+                )
+
+        def activate(g):
+            for h in range(HALVES):
+                activated[g, h] = keep.tile([P, BANK], F32, name="activated%d_%d" % (g, h))
+                nc.scalar.activation(activated[g, h][:], sums[g, h][:], GELU, bias=bias[:, h : h + 1])
+
+        def finish(g):
+            cols = slice(g * BANK, (g + 1) * BANK)
+            for h in range(HALVES):
+                result = keep.tile([P, BANK], F32, name="result%d_%d" % (g, h))
+                nc.vector.tensor_tensor(result[:], activated[g, h][:], picked_residual[h][:, cols], ADD)
+                nc.sync.dma_start(out[h * P : (h + 1) * P, cols], result[:])
+
+        round_piece(0)
+        round_piece(1)
+        multiply_piece(0)
+        multiply_piece(1)
+        round_piece(2)
+        activate(0)
+        round_piece(3)
+        multiply_piece(2)
+        multiply_piece(3)
+        round_piece(4)
+        finish(0)
+        activate(1)
+        round_piece(5)
+        multiply_piece(4)
+        multiply_piece(5)
+        finish(1)
+        activate(2)
+        finish(2)

@@ -22,6 +22,7 @@ HALVES = M // P
 BANK = 512
 PIECE = 256
 VECTOR_PIECES = (3, 5)
+GROUPED_AT = (60, 62, 64, 40, 33, 50)
 
 
 def interleave(copy, grouped, raw):
@@ -37,44 +38,42 @@ def tile_list_tabres_gelu_kernel(
     nc = tc.nc
     with ExitStack() as ctx:
         keep = ctx.enter_context(tc.tile_pool(name="keep", bufs=1))
+        stage = ctx.enter_context(tc.tile_pool(name="stage", bufs=1))
+
+        def staged(shape, dtype, name, kib):
+            return stage.tile(shape, dtype, name=name, align_bytes=64, offset=1024 * kib)
+
         psum = ctx.enter_context(tc.psum_pool(name="psum", bufs=1))
 
         offsets = keep.tile([P, S // 16], U16, name="offsets")
         nc.sync.dma_start(offsets[:], offs)
 
+        w4_codes = keep.tile([P, 2 * M], U8, name="w4_codes", align_bytes=64)
+        nc.sync.dma_start(w4_codes[:].bitcast(I32), w4_words[0].bitcast(I32))
+        table_words = staged([P, T], I32, "table_words", 0)
+        nc.sync.dma_start(table_words[:], tab_words[0].rearrange("p t i -> p (t i)").bitcast(I32))
         table_scales = keep.tile([P, T // 4], I32, name="table_scales")
         nc.vector.memset(table_scales[:], 0)
         w4_plane = keep.tile([P, M // 4], I32, name="w4_plane", align_bytes=64)
-        nc.vector.memset(w4_plane[:], 0)
+        nc.gpsimd.memset(w4_plane[:], 0)
         for q in range(4):
-            nc.gpsimd.dma_start(table_scales[32 * q : 32 * q + 4, :], tab_scales[0, 4 * q : 4 * q + 4, :].bitcast(I32))
+            nc.sync.dma_start(table_scales[32 * q : 32 * q + 4, :], tab_scales[0, 4 * q : 4 * q + 4, :].bitcast(I32))
         for q in range(4):
             nc.gpsimd.dma_start(w4_plane[32 * q : 32 * q + 4, :], w4_scales[0, 4 * q : 4 * q + 4, :].bitcast(I32))
 
-        table_words = keep.tile([P, T], I32, name="table_words")
-        nc.sync.dma_start(table_words[:], tab_words[0].rearrange("p t i -> p (t i)").bitcast(I32))
 
         bias = keep.tile([P, HALVES], F32, name="bias")
         with nc.allow_non_contiguous_dma(reason="one bias value a partition"):
-            nc.scalar.dma_start(bias[:], b.rearrange("(h p) -> p h", p=P))
-        w4_codes = keep.tile([P, 2 * M], U8, name="w4_codes", align_bytes=64)
-        nc.scalar.dma_start(w4_codes[:].bitcast(I32), w4_words[0].bitcast(I32))
-        warm = keep.tile([P, 1], F32, name="warm")
-        nc.scalar.activation(warm[:], bias[:, 0:1], GELU)
+            nc.gpsimd.dma_start(bias[:], b.rearrange("(h p) -> p h", p=P))
+        warm = stage.tile([P, 32], F32, name="warm", align_bytes=64, offset=32 * 1024 - 64)
+        nc.vector.memset(warm[:], 0.0)
+        nc.scalar.activation(warm[:], warm[:], GELU)
 
         residual = []
         for h in range(HALVES):
-            window = keep.tile([P, T], F32, name="residual%d" % h)
+            window = staged([P, T], F32, "residual%d" % h, 16 * (h + 1))
             nc.sync.dma_start(window[:], rT[h * P : (h + 1) * P, :])
             residual.append(window)
-        u_raw = keep.tile([P, PACK, M], F32, name="u_raw")
-        nc.sync.dma_start(u_raw[:], u.rearrange("(p t) n -> p t n", t=PACK))
-        c_rows = c.rearrange("(p t) j -> p t j", t=PACK)
-        c_raw = []
-        for i in range(S // PIECE):
-            raw = keep.tile([P, PACK, PIECE], F32, name="c_raw%d" % i)
-            nc.sync.dma_start(raw[:], c_rows[:, :, i * PIECE : (i + 1) * PIECE])
-            c_raw.append(raw)
 
         picked_scales = keep.tile([P, S], U8, name="picked_scales", align_bytes=64)
         nc.vector.tensor_copy(picked_scales[:], table_scales[:].bitcast(U8).indirect(offsets[:]))
@@ -101,9 +100,18 @@ def tile_list_tabres_gelu_kernel(
                     stop=False,
                 )
 
+        u_raw = staged([P, PACK, M], F32, "u_raw", 0)
+        nc.sync.dma_start(u_raw[:], u.rearrange("(p t) n -> p t n", t=PACK))
+        c_rows = c.rearrange("(p t) j -> p t j", t=PACK)
+        c_raw = []
+        for i in range(S // PIECE):
+            raw = staged([P, PACK, PIECE], F32, "c_raw%d" % i, 4 * (i + 1))
+            nc.sync.dma_start(raw[:], c_rows[:, :, i * PIECE : (i + 1) * PIECE])
+            c_raw.append(raw)
+
         u_grouped = keep.tile([P, PACK * M], BF16, name="u_grouped", align_bytes=64)
         interleave(nc.scalar.copy, u_grouped[:], u_raw[:])
-        u_codes = keep.tile([P, M], U32, name="u_codes", align_bytes=64)
+        u_codes = staged([P, M], U32, "u_codes", 32)
         u_plane = keep.tile([P, M], U8, name="u_plane", align_bytes=64)
         nc.vector.quantize_mx(out=u_codes[:].bitcast(FP8X4), scales=u_plane[:], in_=u_grouped[:])
 
@@ -111,12 +119,12 @@ def tile_list_tabres_gelu_kernel(
         activated = {}
 
         def round_piece(i):
-            grouped[i] = keep.tile([P, PACK * PIECE], BF16, name="c_grouped%d" % i, align_bytes=64)
+            grouped[i] = staged([P, PACK * PIECE], BF16, "c_grouped%d" % i, GROUPED_AT[i])
             copy = nc.vector.tensor_copy if i in VECTOR_PIECES else nc.scalar.copy
             interleave(copy, grouped[i][:], c_raw[i][:])
 
         def multiply_piece(i):
-            codes = keep.tile([P, PIECE], U32, name="c_codes%d" % i, align_bytes=64)
+            codes = staged([P, PIECE], U32, "c_codes%d" % i, 33 + i)
             plane = keep.tile([P, PIECE], U8, name="c_plane%d" % i, align_bytes=64)
             nc.vector.quantize_mx(out=codes[:].bitcast(FP8X4), scales=plane[:], in_=grouped[i][:])
             g, part = divmod(i, BANK // PIECE)
@@ -133,7 +141,7 @@ def tile_list_tabres_gelu_kernel(
 
         def activate(g):
             for h in range(HALVES):
-                activated[g, h] = keep.tile([P, BANK], F32, name="activated%d_%d" % (g, h))
+                activated[g, h] = staged([P, BANK], F32, "activated%d_%d" % (g, h), 48 + 2 * (HALVES * g + h))
                 nc.scalar.activation(activated[g, h][:], sums[g, h][:], GELU, bias=bias[:, h : h + 1])
 
         def finish(g):

@@ -20,9 +20,10 @@ P = 128
 PACK = 4
 HALVES = M // P
 BANK = 512
-PIECE = 256
-VECTOR_PIECES = (3, 5)
-GROUPED_AT = (60, 62, 64, 40, 33, 50)
+BANKS = S // BANK
+C_LOADS = (1024, 512)
+SCALAR_COLUMNS = 256
+SLICES = ((512, 512, 512), (512, 512, 256, 256))
 
 
 def interleave(copy, grouped, raw):
@@ -39,56 +40,67 @@ def tile_list_tabres_gelu_kernel(
     with ExitStack() as ctx:
         keep = ctx.enter_context(tc.tile_pool(name="keep", bufs=1))
         stage = ctx.enter_context(tc.tile_pool(name="stage", bufs=1))
+        psum = ctx.enter_context(tc.psum_pool(name="psum", bufs=1))
 
         def staged(shape, dtype, name, kib):
             return stage.tile(shape, dtype, name=name, align_bytes=64, offset=1024 * kib)
 
-        psum = ctx.enter_context(tc.psum_pool(name="psum", bufs=1))
-
         offsets = keep.tile([P, S // 16], U16, name="offsets")
         nc.sync.dma_start(offsets[:], offs)
 
-        w4_codes = keep.tile([P, 2 * M], U8, name="w4_codes", align_bytes=64)
-        nc.sync.dma_start(w4_codes[:].bitcast(I32), w4_words[0].bitcast(I32))
-        table_words = staged([P, T], I32, "table_words", 0)
-        nc.sync.dma_start(table_words[:], tab_words[0].rearrange("p t i -> p (t i)").bitcast(I32))
-        table_scales = keep.tile([P, T // 4], I32, name="table_scales")
-        nc.vector.memset(table_scales[:], 0)
         w4_plane = keep.tile([P, M // 4], I32, name="w4_plane", align_bytes=64)
         nc.gpsimd.memset(w4_plane[:], 0)
         for q in range(4):
-            nc.sync.dma_start(table_scales[32 * q : 32 * q + 4, :], tab_scales[0, 4 * q : 4 * q + 4, :].bitcast(I32))
-        for q in range(4):
-            nc.gpsimd.dma_start(w4_plane[32 * q : 32 * q + 4, :], w4_scales[0, 4 * q : 4 * q + 4, :].bitcast(I32))
-
-
+            nc.scalar.dma_start(w4_plane[32 * q : 32 * q + 4, :], w4_scales[0, 4 * q : 4 * q + 4, :].bitcast(I32))
+        w4_codes = keep.tile([P, 2 * M], U8, name="w4_codes", align_bytes=64)
+        nc.sync.dma_start(w4_codes[:].bitcast(I32), w4_words[0].bitcast(I32))
         bias = keep.tile([P, HALVES], F32, name="bias")
         with nc.allow_non_contiguous_dma(reason="one bias value a partition"):
-            nc.gpsimd.dma_start(bias[:], b.rearrange("(h p) -> p h", p=P))
-        warm = stage.tile([P, 32], F32, name="warm", align_bytes=64, offset=32 * 1024 - 64)
-        nc.vector.memset(warm[:], 0.0)
-        nc.scalar.activation(warm[:], warm[:], GELU)
+            nc.sync.dma_start(bias[:], b.rearrange("(h p) -> p h", p=P))
 
+        table_words = keep.tile([P, T], I32, name="table_words")
+        nc.sync.dma_start(table_words[:], tab_words[0].rearrange("p t i -> p (t i)").bitcast(I32))
+        table_scales = keep.tile([P, T // 4], I32, name="table_scales")
+        nc.vector.memset(table_scales[:], 0)
+        for q in range(4):
+            nc.sync.dma_start(table_scales[32 * q : 32 * q + 4, :], tab_scales[0, 4 * q : 4 * q + 4, :].bitcast(I32))
+
+        warm = staged([P, 15 * 1024], F32, "warm", 0)
+        nc.vector.memset(warm[:, 0:32], 0.0)
+        nc.scalar.activation(warm[:, 0:32], warm[:, 0:32], GELU)
+
+        u_raw = staged([P, PACK, M], F32, "u_raw", 0)
+        nc.sync.dma_start(u_raw[:], u.rearrange("(p t) n -> p t n", t=PACK))
+        c_rows = c.rearrange("(p t) j -> p t j", t=PACK)
+        c_raw = []
+        first = 0
+        for i, width in enumerate(C_LOADS):
+            raw = staged([P, PACK, width], F32, "c_raw%d" % i, 4 + first // 64)
+            nc.sync.dma_start(raw[:], c_rows[:, :, first : first + width])
+            for g in range(width // BANK):
+                c_raw.append(raw[:, :, g * BANK : (g + 1) * BANK])
+            first = first + width
         residual = []
         for h in range(HALVES):
-            window = staged([P, T], F32, "residual%d" % h, 16 * (h + 1))
+            window = staged([P, T], F32, "residual%d" % h, 28 + 16 * h)
             nc.sync.dma_start(window[:], rT[h * P : (h + 1) * P, :])
             residual.append(window)
 
-        picked_scales = keep.tile([P, S], U8, name="picked_scales", align_bytes=64)
-        nc.vector.tensor_copy(picked_scales[:], table_scales[:].bitcast(U8).indirect(offsets[:]))
         picked_words = keep.tile([P, S], U32, name="picked_words", align_bytes=64)
         nc.vector.tensor_copy(picked_words[:], table_words[:].bitcast(U32).indirect(offsets[:]))
-        picked_residual = []
-        for h in range(HALVES):
-            picked = keep.tile([P, S], F32, name="picked_residual%d" % h)
-            nc.vector.tensor_copy(picked[:], residual[h][:].indirect(offsets[:]))
-            picked_residual.append(picked)
+        picked_scales = keep.tile([P, S], U8, name="picked_scales", align_bytes=64)
+        nc.vector.tensor_copy(picked_scales[:], table_scales[:].bitcast(U8).indirect(offsets[:]))
+
+        u_grouped = keep.tile([P, PACK * M], BF16, name="u_grouped", align_bytes=64)
+        interleave(nc.scalar.copy, u_grouped[:], u_raw[:])
+        u_codes = keep.tile([P, M], U32, name="u_codes", align_bytes=64)
+        u_plane = keep.tile([P, M], U8, name="u_plane", align_bytes=64)
+        nc.vector.quantize_mx(out=u_codes[:].bitcast(FP8X4), scales=u_plane[:], in_=u_grouped[:])
 
         sums = {}
-        for g in range(S // BANK):
+        for g in range(BANKS):
+            cols = slice(g * BANK, (g + 1) * BANK)
             for h in range(HALVES):
-                cols = slice(g * BANK, (g + 1) * BANK)
                 sums[g, h] = psum.tile([P, BANK], F32, name="sum%d_%d" % (g, h))
                 nc.tensor.matmul_mx(
                     out=sums[g, h][:],
@@ -100,72 +112,36 @@ def tile_list_tabres_gelu_kernel(
                     stop=False,
                 )
 
-        u_raw = staged([P, PACK, M], F32, "u_raw", 0)
-        nc.sync.dma_start(u_raw[:], u.rearrange("(p t) n -> p t n", t=PACK))
-        c_rows = c.rearrange("(p t) j -> p t j", t=PACK)
-        c_raw = []
-        for i in range(S // PIECE):
-            raw = staged([P, PACK, PIECE], F32, "c_raw%d" % i, 4 * (i + 1))
-            nc.sync.dma_start(raw[:], c_rows[:, :, i * PIECE : (i + 1) * PIECE])
-            c_raw.append(raw)
-
-        u_grouped = keep.tile([P, PACK * M], BF16, name="u_grouped", align_bytes=64)
-        interleave(nc.scalar.copy, u_grouped[:], u_raw[:])
-        u_codes = staged([P, M], U32, "u_codes", 32)
-        u_plane = keep.tile([P, M], U8, name="u_plane", align_bytes=64)
-        nc.vector.quantize_mx(out=u_codes[:].bitcast(FP8X4), scales=u_plane[:], in_=u_grouped[:])
-
-        grouped = {}
-        activated = {}
-
-        def round_piece(i):
-            grouped[i] = staged([P, PACK * PIECE], BF16, "c_grouped%d" % i, GROUPED_AT[i])
-            copy = nc.vector.tensor_copy if i in VECTOR_PIECES else nc.scalar.copy
-            interleave(copy, grouped[i][:], c_raw[i][:])
-
-        def multiply_piece(i):
-            codes = staged([P, PIECE], U32, "c_codes%d" % i, 33 + i)
-            plane = keep.tile([P, PIECE], U8, name="c_plane%d" % i, align_bytes=64)
-            nc.vector.quantize_mx(out=codes[:].bitcast(FP8X4), scales=plane[:], in_=grouped[i][:])
-            g, part = divmod(i, BANK // PIECE)
+        grouped = []
+        for g in range(BANKS):
+            tile = keep.tile([P, PACK * BANK], BF16, name="c_grouped%d" % g, align_bytes=64)
+            interleave(nc.scalar.copy, tile[:, 0 : PACK * SCALAR_COLUMNS], c_raw[g][:, :, 0:SCALAR_COLUMNS])
+            interleave(nc.vector.tensor_copy, tile[:, PACK * SCALAR_COLUMNS :], c_raw[g][:, :, SCALAR_COLUMNS:])
+            grouped.append(tile)
+        for g in range(BANKS):
+            codes = keep.tile([P, BANK], U32, name="c_codes%d" % g, align_bytes=64)
+            plane = keep.tile([P, BANK], U8, name="c_plane%d" % g, align_bytes=64)
+            nc.vector.quantize_mx(out=codes[:].bitcast(FP8X4), scales=plane[:], in_=grouped[g][:])
             for h in range(HALVES):
                 nc.tensor.matmul_mx(
-                    out=sums[g, h][:, part * PIECE : (part + 1) * PIECE],
+                    out=sums[g, h][:],
                     lhsT=u_codes[:, h * P : (h + 1) * P].bitcast(FP8X4),
                     lhsT_scale=u_plane[:, h * P : (h + 1) * P],
                     rhs=codes[:].bitcast(FP8X4),
                     rhs_scale=plane[:],
                     start=False,
-                    stop=(part == BANK // PIECE - 1),
+                    stop=True,
                 )
 
-        def activate(g):
-            for h in range(HALVES):
-                activated[g, h] = staged([P, BANK], F32, "activated%d_%d" % (g, h), 48 + 2 * (HALVES * g + h))
-                nc.scalar.activation(activated[g, h][:], sums[g, h][:], GELU, bias=bias[:, h : h + 1])
-
-        def finish(g):
-            cols = slice(g * BANK, (g + 1) * BANK)
-            for h in range(HALVES):
-                result = keep.tile([P, BANK], F32, name="result%d_%d" % (g, h))
-                nc.vector.tensor_tensor(result[:], activated[g, h][:], picked_residual[h][:, cols], ADD)
+        for h in range(HALVES):
+            activated = keep.tile([P, S], F32, name="activated%d" % h)
+            for g in range(BANKS):
+                nc.scalar.activation(activated[:, g * BANK : (g + 1) * BANK], sums[g, h][:], GELU, bias=bias[:, h : h + 1])
+            first = 0
+            for i, width in enumerate(SLICES[h]):
+                cols = slice(first, first + width)
+                result = keep.tile([P, width], F32, name="result%d_%d" % (h, i))
+                picked = residual[h][:].indirect(offsets[:, first // 16 : (first + width) // 16])
+                nc.vector.tensor_tensor(result[:], picked, activated[:, cols], ADD)
                 nc.sync.dma_start(out[h * P : (h + 1) * P, cols], result[:])
-
-        round_piece(0)
-        round_piece(1)
-        multiply_piece(0)
-        multiply_piece(1)
-        round_piece(2)
-        activate(0)
-        round_piece(3)
-        multiply_piece(2)
-        multiply_piece(3)
-        round_piece(4)
-        finish(0)
-        activate(1)
-        round_piece(5)
-        multiply_piece(4)
-        multiply_piece(5)
-        finish(1)
-        activate(2)
-        finish(2)
+                first = first + width

@@ -21,7 +21,6 @@ PACK = 4
 HALVES = M // P
 BANK = 512
 BANKS = S // BANK
-C_LOADS = (1024, 512)
 SCALAR_COLUMNS = 256
 SLICES = ((512, 512, 512), (512, 512, 256, 256))
 
@@ -50,8 +49,8 @@ def tile_list_tabres_gelu_kernel(
 
         w4_plane = keep.tile([P, M // 4], I32, name="w4_plane", align_bytes=64)
         nc.gpsimd.memset(w4_plane[:], 0)
-        for q in range(4):
-            nc.scalar.dma_start(w4_plane[32 * q : 32 * q + 4, :], w4_scales[0, 4 * q : 4 * q + 4, :].bitcast(I32))
+        for r in range(4):
+            nc.scalar.dma_start(w4_plane[r:P:32, :], w4_scales[0].bitcast(I32)[r:16:4, :])
         w4_codes = keep.tile([P, 2 * M], U8, name="w4_codes", align_bytes=64)
         nc.sync.dma_start(w4_codes[:].bitcast(I32), w4_words[0].bitcast(I32))
         bias = keep.tile([P, HALVES], F32, name="bias")
@@ -62,24 +61,18 @@ def tile_list_tabres_gelu_kernel(
         nc.sync.dma_start(table_words[:], tab_words[0].rearrange("p t i -> p (t i)").bitcast(I32))
         table_scales = keep.tile([P, T // 4], I32, name="table_scales")
         nc.vector.memset(table_scales[:], 0)
-        for q in range(4):
-            nc.sync.dma_start(table_scales[32 * q : 32 * q + 4, :], tab_scales[0, 4 * q : 4 * q + 4, :].bitcast(I32))
+        for r in range(4):
+            nc.sync.dma_start(table_scales[r:P:32, :], tab_scales[0].bitcast(I32)[r:16:4, :])
 
         warm = staged([P, 15 * 1024], F32, "warm", 0)
         nc.vector.memset(warm[:, 0:32], 0.0)
         nc.scalar.activation(warm[:, 0:32], warm[:, 0:32], GELU)
 
+        c_whole = staged([P, PACK, S], F32, "c_whole", 4)
+        nc.sync.dma_start(c_whole[:], c.rearrange("(p t) j -> p t j", t=PACK))
+        c_raw = [c_whole[:, :, g * BANK : (g + 1) * BANK] for g in range(BANKS)]
         u_raw = staged([P, PACK, M], F32, "u_raw", 0)
         nc.sync.dma_start(u_raw[:], u.rearrange("(p t) n -> p t n", t=PACK))
-        c_rows = c.rearrange("(p t) j -> p t j", t=PACK)
-        c_raw = []
-        first = 0
-        for i, width in enumerate(C_LOADS):
-            raw = staged([P, PACK, width], F32, "c_raw%d" % i, 4 + first // 64)
-            nc.sync.dma_start(raw[:], c_rows[:, :, first : first + width])
-            for g in range(width // BANK):
-                c_raw.append(raw[:, :, g * BANK : (g + 1) * BANK])
-            first = first + width
         residual = []
         for h in range(HALVES):
             window = staged([P, T], F32, "residual%d" % h, 28 + 16 * h)

@@ -38,11 +38,7 @@ def tile_list_tabres_gelu_kernel(
     nc = tc.nc
     with ExitStack() as ctx:
         keep = ctx.enter_context(tc.tile_pool(name="keep", bufs=1))
-        stage = ctx.enter_context(tc.tile_pool(name="stage", bufs=1))
         psum = ctx.enter_context(tc.psum_pool(name="psum", bufs=1))
-
-        def staged(shape, dtype, name, kib):
-            return stage.tile(shape, dtype, name=name, align_bytes=64, offset=1024 * kib)
 
         offsets = keep.tile([P, S // 16], U16, name="offsets")
         nc.sync.dma_start(offsets[:], offs)
@@ -57,32 +53,37 @@ def tile_list_tabres_gelu_kernel(
         with nc.allow_non_contiguous_dma(reason="one bias value a partition"):
             nc.sync.dma_start(bias[:], b.rearrange("(h p) -> p h", p=P))
 
-        table_words = keep.tile([P, T], I32, name="table_words")
+        table_words = keep.tile([P, T], I32, name="table_words", tag="words_then_residual")
         nc.sync.dma_start(table_words[:], tab_words[0].rearrange("p t i -> p (t i)").bitcast(I32))
-        table_scales = keep.tile([P, T // 4], I32, name="table_scales")
+        u_raw = keep.tile([P, PACK, M], F32, name="u_raw")
+        nc.sync.dma_start(u_raw[:], u.rearrange("(p t) n -> p t n", t=PACK))
+        table_scales = keep.tile([P, T // 4], I32, name="table_scales", tag="scales_then_residual")
         nc.vector.memset(table_scales[:], 0)
-        for r in range(4):
-            nc.sync.dma_start(table_scales[r:P:32, :], tab_scales[0].bitcast(I32)[r:16:4, :])
+        nc.scalar.dma_start(table_scales[32:96:4, :], tab_scales[0].bitcast(I32))
+        scale_plane = keep.tile([P, S // 4], I32, name="scale_plane", align_bytes=64)
+        nc.vector.memset(scale_plane[:], 0)
 
-        warm = staged([P, 15 * 1024], F32, "warm", 0)
-        nc.vector.memset(warm[:, 0:32], 0.0)
-        nc.scalar.activation(warm[:, 0:32], warm[:, 0:32], GELU)
+        warm = keep.tile([P, 32], F32, name="warm", tag="warm_then_c")
+        nc.vector.memset(warm[:], 0.0)
+        nc.scalar.activation(warm[:], warm[:], GELU)
 
-        c_whole = staged([P, PACK, S], F32, "c_whole", 4)
+        c_whole = keep.tile([P, PACK, S], F32, name="c_whole", tag="warm_then_c")
         nc.sync.dma_start(c_whole[:], c.rearrange("(p t) j -> p t j", t=PACK))
         c_raw = [c_whole[:, :, g * BANK : (g + 1) * BANK] for g in range(BANKS)]
-        u_raw = staged([P, PACK, M], F32, "u_raw", 0)
-        nc.sync.dma_start(u_raw[:], u.rearrange("(p t) n -> p t n", t=PACK))
-        residual = []
-        for h in range(HALVES):
-            window = staged([P, T], F32, "residual%d" % h, 28 + 16 * h)
-            nc.sync.dma_start(window[:], rT[h * P : (h + 1) * P, :])
-            residual.append(window)
 
+        picked_rows = keep.tile([P, S], U8, name="picked_rows")
+        nc.vector.tensor_copy(picked_rows[:], table_scales[:].bitcast(U8).indirect(offsets[:]))
+        for r in range(4):
+            nc.sync.dma_start(scale_plane[r:P:32, :], picked_rows[:].bitcast(I32)[32 + 4 * r : 96 : 16, :])
+        picked_scales = scale_plane[:].bitcast(U8)
         picked_words = keep.tile([P, S], U32, name="picked_words", align_bytes=64)
         nc.vector.tensor_copy(picked_words[:], table_words[:].bitcast(U32).indirect(offsets[:]))
-        picked_scales = keep.tile([P, S], U8, name="picked_scales", align_bytes=64)
-        nc.vector.tensor_copy(picked_scales[:], table_scales[:].bitcast(U8).indirect(offsets[:]))
+
+        residual = []
+        for h, tag in enumerate(("scales_then_residual", "words_then_residual")):
+            window = keep.tile([P, T], F32, name="residual%d" % h, tag=tag)
+            nc.sync.dma_start(window[:], rT[h * P : (h + 1) * P, :])
+            residual.append(window)
 
         u_grouped = keep.tile([P, PACK * M], BF16, name="u_grouped", align_bytes=64)
         interleave(nc.scalar.copy, u_grouped[:], u_raw[:])

@@ -42,69 +42,47 @@ def tile_list_tabres_gelu_kernel(
 
         offsets = keep.tile([P, S // 16], U16, name="offsets")
         nc.sync.dma_start(offsets[:], offs)
+        u_raw = keep.tile([P, PACK, M], F32, name="u_raw")
+        nc.sync.dma_start(u_raw[:], u.rearrange("(p t) n -> p t n", t=PACK))
 
-        w4_plane = keep.tile([P, M // 4], I32, name="w4_plane", align_bytes=64)
-        nc.gpsimd.memset(w4_plane[:], 0)
-        for r in range(4):
-            nc.scalar.dma_start(w4_plane[r:P:32, :], w4_scales[0].bitcast(I32)[r:16:4, :])
+        scale_rows = keep.tile([P, (S + M) // 4], I32, name="scale_rows")
+        nc.sync.dma_start(scale_rows[32:96:4, S // 4 :], w4_scales[0].bitcast(I32))
         w4_codes = keep.tile([P, 2 * M], U8, name="w4_codes", align_bytes=64)
         nc.sync.dma_start(w4_codes[:].bitcast(I32), w4_words[0].bitcast(I32))
         bias = keep.tile([P, HALVES], F32, name="bias")
         with nc.allow_non_contiguous_dma(reason="one bias value a partition"):
             nc.sync.dma_start(bias[:], b.rearrange("(h p) -> p h", p=P))
 
-        table_words = keep.tile([P, T], I32, name="table_words", tag="words_then_residual")
-        nc.sync.dma_start(table_words[:], tab_words[0].rearrange("p t i -> p (t i)").bitcast(I32))
-        u_raw = keep.tile([P, PACK, M], F32, name="u_raw")
-        nc.sync.dma_start(u_raw[:], u.rearrange("(p t) n -> p t n", t=PACK))
-        table_scales = keep.tile([P, T // 4], I32, name="table_scales", tag="scales_then_residual")
-        nc.vector.memset(table_scales[:], 0)
-        nc.scalar.dma_start(table_scales[32:96:4, :], tab_scales[0].bitcast(I32))
-        scale_plane = keep.tile([P, S // 4], I32, name="scale_plane", align_bytes=64)
+        table_scales = keep.tile([P, T // 4], I32, name="table_scales", tag="scales_then_u", align_bytes=64)
+        nc.gpsimd.memset(table_scales[:], 0)
+        nc.sync.dma_start(table_scales[32:96:4, :], tab_scales[0].bitcast(I32))
+        scale_plane = keep.tile([P, (S + M) // 4], I32, name="scale_plane", align_bytes=64)
         nc.vector.memset(scale_plane[:], 0)
 
-        warm = keep.tile([P, 32], F32, name="warm", tag="warm_then_c")
+        warm = keep.tile([P, 32], F32, name="warm")
         nc.vector.memset(warm[:], 0.0)
         nc.scalar.activation(warm[:], warm[:], GELU)
 
-        c_whole = keep.tile([P, PACK, S], F32, name="c_whole", tag="warm_then_c")
+        c_whole = keep.tile([P, PACK, S], F32, name="c_whole", tag="c_then_residual")
         nc.sync.dma_start(c_whole[:], c.rearrange("(p t) j -> p t j", t=PACK))
         c_raw = [c_whole[:, :, g * BANK : (g + 1) * BANK] for g in range(BANKS)]
 
-        picked_rows = keep.tile([P, S], U8, name="picked_rows")
+        table_words = keep.tile([P, T], I32, name="table_words")
+        nc.sync.dma_start(table_words[:], tab_words[0].rearrange("p t i -> p (t i)").bitcast(I32))
+
+        picked_rows = keep.tile([P, S], U8, name="picked_rows", tag="rows_then_residual")
         nc.vector.tensor_copy(picked_rows[:], table_scales[:].bitcast(U8).indirect(offsets[:]))
+        nc.vector.tensor_copy(scale_rows[:, 0 : S // 4], picked_rows[:].bitcast(I32))
         for r in range(4):
-            nc.sync.dma_start(scale_plane[r:P:32, :], picked_rows[:].bitcast(I32)[32 + 4 * r : 96 : 16, :])
-        picked_scales = scale_plane[:].bitcast(U8)
-        picked_words = keep.tile([P, S], U32, name="picked_words", align_bytes=64)
-        nc.vector.tensor_copy(picked_words[:], table_words[:].bitcast(U32).indirect(offsets[:]))
+            nc.sync.dma_start(scale_plane[r:P:32, :], scale_rows[32 + 4 * r : 96 : 16, :])
+        picked_scales = scale_plane[:].bitcast(U8)[:, 0:S]
+        w4_plane = scale_plane[:].bitcast(U8)[:, S:]
 
-        residual = []
-        for h, tag in enumerate(("scales_then_residual", "words_then_residual")):
-            window = keep.tile([P, T], F32, name="residual%d" % h, tag=tag)
-            nc.sync.dma_start(window[:], rT[h * P : (h + 1) * P, :])
-            residual.append(window)
-
-        u_grouped = keep.tile([P, PACK * M], BF16, name="u_grouped", align_bytes=64)
+        u_grouped = keep.tile([P, PACK * M], BF16, name="u_grouped", tag="scales_then_u", align_bytes=64)
         interleave(nc.scalar.copy, u_grouped[:], u_raw[:])
         u_codes = keep.tile([P, M], U32, name="u_codes", align_bytes=64)
         u_plane = keep.tile([P, M], U8, name="u_plane", align_bytes=64)
         nc.vector.quantize_mx(out=u_codes[:].bitcast(FP8X4), scales=u_plane[:], in_=u_grouped[:])
-
-        sums = {}
-        for g in range(BANKS):
-            cols = slice(g * BANK, (g + 1) * BANK)
-            for h in range(HALVES):
-                sums[g, h] = psum.tile([P, BANK], F32, name="sum%d_%d" % (g, h))
-                nc.tensor.matmul_mx(
-                    out=sums[g, h][:],
-                    lhsT=w4_codes[:, 2 * h * P : 2 * (h + 1) * P].bitcast(FP4X4),
-                    lhsT_scale=w4_plane[:].bitcast(U8)[:, h * P : (h + 1) * P],
-                    rhs=picked_words[:, cols].bitcast(FP8X4),
-                    rhs_scale=picked_scales[:, cols],
-                    start=True,
-                    stop=False,
-                )
 
         grouped = []
         for g in range(BANKS):
@@ -112,17 +90,42 @@ def tile_list_tabres_gelu_kernel(
             interleave(nc.scalar.copy, tile[:, 0 : PACK * SCALAR_COLUMNS], c_raw[g][:, :, 0:SCALAR_COLUMNS])
             interleave(nc.vector.tensor_copy, tile[:, PACK * SCALAR_COLUMNS :], c_raw[g][:, :, SCALAR_COLUMNS:])
             grouped.append(tile)
+
+        residual = []
+        for h, tag in enumerate(("rows_then_residual", "c_then_residual")):
+            window = keep.tile([P, T], F32, name="residual%d" % h, tag=tag)
+            nc.sync.dma_start(window[:], rT[h * P : (h + 1) * P, :])
+            residual.append(window)
+
+        sums = {}
         for g in range(BANKS):
             codes = keep.tile([P, BANK], U32, name="c_codes%d" % g, align_bytes=64)
             plane = keep.tile([P, BANK], U8, name="c_plane%d" % g, align_bytes=64)
             nc.vector.quantize_mx(out=codes[:].bitcast(FP8X4), scales=plane[:], in_=grouped[g][:])
             for h in range(HALVES):
+                sums[g, h] = psum.tile([P, BANK], F32, name="sum%d_%d" % (g, h))
                 nc.tensor.matmul_mx(
                     out=sums[g, h][:],
                     lhsT=u_codes[:, h * P : (h + 1) * P].bitcast(FP8X4),
                     lhsT_scale=u_plane[:, h * P : (h + 1) * P],
                     rhs=codes[:].bitcast(FP8X4),
                     rhs_scale=plane[:],
+                    start=True,
+                    stop=False,
+                )
+
+        for g in range(BANKS):
+            cols = slice(g * BANK, (g + 1) * BANK)
+            picked_words = keep.tile([P, BANK], U32, name="picked_words%d" % g, align_bytes=64)
+            listed = offsets[:, g * BANK // 16 : (g + 1) * BANK // 16]
+            nc.vector.tensor_copy(picked_words[:], table_words[:].bitcast(U32).indirect(listed))
+            for h in range(HALVES):
+                nc.tensor.matmul_mx(
+                    out=sums[g, h][:],
+                    lhsT=w4_codes[:, 2 * h * P : 2 * (h + 1) * P].bitcast(FP4X4),
+                    lhsT_scale=w4_plane[:, h * P : (h + 1) * P],
+                    rhs=picked_words[:].bitcast(FP8X4),
+                    rhs_scale=picked_scales[:, cols],
                     start=False,
                     stop=True,
                 )

@@ -1,6 +1,7 @@
 from contextlib import ExitStack
 
 import concourse.mybir as mybir
+from concourse.masks import make_identity
 
 K, M, T, S = 512, 256, 4096, 1536
 FLOPS = 2 * 2 * K * M * S
@@ -22,7 +23,7 @@ HALVES = M // P
 BANK = 512
 BANKS = S // BANK
 SCALAR_COLUMNS = 256
-SLICES = ((512, 512, 512), (512, 512, 256, 256))
+SLICES = ((512, 512, 512), (512, 512, 384, 128))
 
 
 def interleave(copy, grouped, raw):
@@ -49,13 +50,20 @@ def tile_list_tabres_gelu_kernel(
         nc.sync.dma_start(scale_rows[32:96:4, S // 4 :], w4_scales[0].bitcast(I32))
         w4_codes = keep.tile([P, 2 * M], U8, name="w4_codes", align_bytes=64)
         nc.sync.dma_start(w4_codes[:].bitcast(I32), w4_words[0].bitcast(I32))
-        bias = keep.tile([P, HALVES], F32, name="bias")
-        with nc.allow_non_contiguous_dma(reason="one bias value a partition"):
-            nc.sync.dma_start(bias[:], b.rearrange("(h p) -> p h", p=P))
-
         table_scales = keep.tile([P, T // 4], I32, name="table_scales", tag="scales_then_u", align_bytes=64)
-        nc.gpsimd.memset(table_scales[:], 0)
+        nc.vector.memset(table_scales[:], 0)
         nc.sync.dma_start(table_scales[32:96:4, :], tab_scales[0].bitcast(I32))
+
+        bias_rows = keep.tile([P, P], F32, name="bias_rows")
+        nc.vector.memset(bias_rows[:], 0.0)
+        nc.scalar.dma_start(bias_rows[0:HALVES, :], b.rearrange("(h p) -> h p", p=P))
+        identity = keep.tile([P, P], F32, name="identity")
+        make_identity(nc, identity[:])
+        bias_turned = psum.tile([P, P], F32, name="bias_turned")
+        nc.tensor.transpose(bias_turned[:], bias_rows[:], identity[:])
+        bias = keep.tile([P, HALVES], F32, name="bias")
+        nc.scalar.copy(bias[:], bias_turned[:, 0:HALVES])
+
         scale_plane = keep.tile([P, (S + M) // 4], I32, name="scale_plane", align_bytes=64)
         nc.vector.memset(scale_plane[:], 0)
 

@@ -58,7 +58,8 @@ def tile_list_tabres_gelu_kernel(
         nc.vector.memset(bias_rows[:], 0.0)
         nc.scalar.dma_start(bias_rows[0:HALVES, :], b.rearrange("(h p) -> h p", p=P))
         identity = keep.tile([P, P], F32, name="identity")
-        make_identity(nc, identity[:])
+        nc.vector.memset(identity[:], 0.0)
+        make_identity(nc, identity[:], nomemset=True)
         bias_turned = psum.tile([P, P], F32, name="bias_turned")
         nc.tensor.transpose(bias_turned[:], bias_rows[:], identity[:])
         bias = keep.tile([P, HALVES], F32, name="bias")

@@ -23,7 +23,7 @@ HALVES = M // P
 BANK = 512
 BANKS = S // BANK
 SCALAR_COLUMNS = 256
-SLICES = ((512, 512, 512), (512, 512, 384, 128))
+SLICES = ((512, 512, 512), (640, 512, 256, 128))
 
 
 def interleave(copy, grouped, raw):
@@ -67,10 +67,6 @@ def tile_list_tabres_gelu_kernel(
 
         scale_plane = keep.tile([P, (S + M) // 4], I32, name="scale_plane", align_bytes=64)
         nc.vector.memset(scale_plane[:], 0)
-
-        warm = keep.tile([P, 32], F32, name="warm")
-        nc.vector.memset(warm[:], 0.0)
-        nc.scalar.activation(warm[:], warm[:], GELU)
 
         c_whole = keep.tile([P, PACK, S], F32, name="c_whole", tag="c_then_residual")
         nc.sync.dma_start(c_whole[:], c.rearrange("(p t) j -> p t j", t=PACK))
@@ -149,5 +145,6 @@ def tile_list_tabres_gelu_kernel(
                 result = keep.tile([P, width], F32, name="result%d_%d" % (h, i))
                 picked = residual[h][:].indirect(offsets[:, first // 16 : (first + width) // 16])
                 nc.vector.tensor_tensor(result[:], picked, activated[:, cols], ADD)
-                nc.sync.dma_start(out[h * P : (h + 1) * P, cols], result[:])
+                queue = nc.scalar if (h, first + width) == (HALVES - 1, S) else nc.sync
+                queue.dma_start(out[h * P : (h + 1) * P, cols], result[:])
                 first = first + width

@@ -43,18 +43,18 @@ def tile_list_tabres_gelu_kernel(
 
         offsets = keep.tile([P, S // 16], U16, name="offsets")
         nc.sync.dma_start(offsets[:], offs)
-        u_raw = keep.tile([P, PACK, M], F32, name="u_raw")
+        u_raw = keep.tile([P, PACK, M], F32, name="u_raw", align_bytes=256)
         nc.sync.dma_start(u_raw[:], u.rearrange("(p t) n -> p t n", t=PACK))
 
-        scale_rows = keep.tile([P, (S + M) // 4], I32, name="scale_rows")
+        scale_rows = keep.tile([P, (S + M) // 4], I32, name="scale_rows", align_bytes=256)
         nc.sync.dma_start(scale_rows[32:96:4, S // 4 :], w4_scales[0].bitcast(I32))
-        w4_codes = keep.tile([P, 2 * M], U8, name="w4_codes", align_bytes=64)
+        w4_codes = keep.tile([P, 2 * M], U8, name="w4_codes", align_bytes=256)
         nc.sync.dma_start(w4_codes[:].bitcast(I32), w4_words[0].bitcast(I32))
-        table_scales = keep.tile([P, T // 4], I32, name="table_scales", tag="scales_then_u", align_bytes=64)
+        table_scales = keep.tile([P, T // 4], I32, name="table_scales", tag="scales_then_u", align_bytes=256)
         nc.vector.memset(table_scales[:], 0)
         nc.sync.dma_start(table_scales[32:96:4, :], tab_scales[0].bitcast(I32))
 
-        bias_rows = keep.tile([P, P], F32, name="bias_rows")
+        bias_rows = keep.tile([P, P], F32, name="bias_rows", align_bytes=256)
         nc.vector.memset(bias_rows[:], 0.0)
         nc.scalar.dma_start(bias_rows[0:HALVES, :], b.rearrange("(h p) -> h p", p=P))
         identity = keep.tile([P, P], F32, name="identity")
@@ -65,17 +65,17 @@ def tile_list_tabres_gelu_kernel(
         bias = keep.tile([P, HALVES], F32, name="bias")
         nc.scalar.copy(bias[:], bias_turned[:, 0:HALVES])
 
-        scale_plane = keep.tile([P, (S + M) // 4], I32, name="scale_plane", align_bytes=64)
+        scale_plane = keep.tile([P, (S + M) // 4], I32, name="scale_plane", align_bytes=256)
         nc.vector.memset(scale_plane[:], 0)
 
-        c_whole = keep.tile([P, PACK, S], F32, name="c_whole", tag="c_then_residual")
+        c_whole = keep.tile([P, PACK, S], F32, name="c_whole", tag="c_then_residual", align_bytes=256)
         nc.sync.dma_start(c_whole[:], c.rearrange("(p t) j -> p t j", t=PACK))
         c_raw = [c_whole[:, :, g * BANK : (g + 1) * BANK] for g in range(BANKS)]
 
-        table_words = keep.tile([P, T], I32, name="table_words")
+        table_words = keep.tile([P, T], I32, name="table_words", align_bytes=256)
         nc.sync.dma_start(table_words[:], tab_words[0].rearrange("p t i -> p (t i)").bitcast(I32))
 
-        picked_rows = keep.tile([P, S], U8, name="picked_rows", tag="rows_then_residual")
+        picked_rows = keep.tile([P, S], U8, name="picked_rows", tag="rows_then_residual", align_bytes=256)
         nc.vector.tensor_copy(picked_rows[:], table_scales[:].bitcast(U8).indirect(offsets[:]))
         nc.vector.tensor_copy(scale_rows[:, 0 : S // 4], picked_rows[:].bitcast(I32))
         for r in range(4):
@@ -83,29 +83,29 @@ def tile_list_tabres_gelu_kernel(
         picked_scales = scale_plane[:].bitcast(U8)[:, 0:S]
         w4_plane = scale_plane[:].bitcast(U8)[:, S:]
 
-        u_grouped = keep.tile([P, PACK * M], BF16, name="u_grouped", tag="scales_then_u", align_bytes=64)
+        u_grouped = keep.tile([P, PACK * M], BF16, name="u_grouped", tag="scales_then_u", align_bytes=256)
         interleave(nc.scalar.copy, u_grouped[:], u_raw[:])
-        u_codes = keep.tile([P, M], U32, name="u_codes", align_bytes=64)
-        u_plane = keep.tile([P, M], U8, name="u_plane", align_bytes=64)
+        u_codes = keep.tile([P, M], U32, name="u_codes", align_bytes=256)
+        u_plane = keep.tile([P, M], U8, name="u_plane", align_bytes=256)
         nc.vector.quantize_mx(out=u_codes[:].bitcast(FP8X4), scales=u_plane[:], in_=u_grouped[:])
 
         grouped = []
         for g in range(BANKS):
-            tile = keep.tile([P, PACK * BANK], BF16, name="c_grouped%d" % g, align_bytes=64)
+            tile = keep.tile([P, PACK * BANK], BF16, name="c_grouped%d" % g, align_bytes=256)
             interleave(nc.scalar.copy, tile[:, 0 : PACK * SCALAR_COLUMNS], c_raw[g][:, :, 0:SCALAR_COLUMNS])
             interleave(nc.vector.tensor_copy, tile[:, PACK * SCALAR_COLUMNS :], c_raw[g][:, :, SCALAR_COLUMNS:])
             grouped.append(tile)
 
         residual = []
         for h, tag in enumerate(("rows_then_residual", "c_then_residual")):
-            window = keep.tile([P, T], F32, name="residual%d" % h, tag=tag)
+            window = keep.tile([P, T], F32, name="residual%d" % h, tag=tag, align_bytes=256)
             nc.sync.dma_start(window[:], rT[h * P : (h + 1) * P, :])
             residual.append(window)
 
         sums = {}
         for g in range(BANKS):
-            codes = keep.tile([P, BANK], U32, name="c_codes%d" % g, align_bytes=64)
-            plane = keep.tile([P, BANK], U8, name="c_plane%d" % g, align_bytes=64)
+            codes = keep.tile([P, BANK], U32, name="c_codes%d" % g, align_bytes=256)
+            plane = keep.tile([P, BANK], U8, name="c_plane%d" % g, align_bytes=256)
             nc.vector.quantize_mx(out=codes[:].bitcast(FP8X4), scales=plane[:], in_=grouped[g][:])
             for h in range(HALVES):
                 sums[g, h] = psum.tile([P, BANK], F32, name="sum%d_%d" % (g, h))
@@ -121,7 +121,7 @@ def tile_list_tabres_gelu_kernel(
 
         for g in range(BANKS):
             cols = slice(g * BANK, (g + 1) * BANK)
-            picked_words = keep.tile([P, BANK], U32, name="picked_words%d" % g, align_bytes=64)
+            picked_words = keep.tile([P, BANK], U32, name="picked_words%d" % g, align_bytes=256)
             listed = offsets[:, g * BANK // 16 : (g + 1) * BANK // 16]
             nc.vector.tensor_copy(picked_words[:], table_words[:].bitcast(U32).indirect(listed))
             for h in range(HALVES):
@@ -142,9 +142,8 @@ def tile_list_tabres_gelu_kernel(
             first = 0
             for i, width in enumerate(SLICES[h]):
                 cols = slice(first, first + width)
-                result = keep.tile([P, width], F32, name="result%d_%d" % (h, i))
+                result = keep.tile([P, width], F32, name="result%d_%d" % (h, i), align_bytes=256)
                 picked = residual[h][:].indirect(offsets[:, first // 16 : (first + width) // 16])
                 nc.vector.tensor_tensor(result[:], picked, activated[:, cols], ADD)
-                queue = nc.scalar if (h, first + width) == (HALVES - 1, S) else nc.sync
-                queue.dma_start(out[h * P : (h + 1) * P, cols], result[:])
+                nc.sync.dma_start(out[h * P : (h + 1) * P, cols], result[:])
                 first = first + width

@@ -22,7 +22,7 @@ PACK = 4
 HALVES = M // P
 BANK = 512
 BANKS = S // BANK
-SCALAR_COLUMNS = 256
+SCALAR_COLUMNS = (0, 128, 512)
 SLICES = ((512, 512, 512), (640, 512, 256, 128))
 
 
@@ -92,8 +92,11 @@ def tile_list_tabres_gelu_kernel(
         grouped = []
         for g in range(BANKS):
             tile = keep.tile([P, PACK * BANK], BF16, name="c_grouped%d" % g, align_bytes=256)
-            interleave(nc.scalar.copy, tile[:, 0 : PACK * SCALAR_COLUMNS], c_raw[g][:, :, 0:SCALAR_COLUMNS])
-            interleave(nc.vector.tensor_copy, tile[:, PACK * SCALAR_COLUMNS :], c_raw[g][:, :, SCALAR_COLUMNS:])
+            split = SCALAR_COLUMNS[g]
+            if split > 0:
+                interleave(nc.scalar.copy, tile[:, 0 : PACK * split], c_raw[g][:, :, 0:split])
+            if split < BANK:
+                interleave(nc.vector.tensor_copy, tile[:, PACK * split :], c_raw[g][:, :, split:])
             grouped.append(tile)
 
         residual = []

@@ -78,8 +78,8 @@ def tile_list_tabres_gelu_kernel(
         picked_rows = keep.tile([P, S], U8, name="picked_rows", tag="rows_then_residual", align_bytes=256)
         nc.vector.tensor_copy(picked_rows[:], table_scales[:].bitcast(U8).indirect(offsets[:]))
         nc.vector.tensor_copy(scale_rows[:, 0 : S // 4], picked_rows[:].bitcast(I32))
-        for r in range(4):
-            nc.sync.dma_start(scale_plane[r:P:32, :], scale_rows[32 + 4 * r : 96 : 16, :])
+        for q in range(4):
+            nc.sync.dma_start(scale_plane[32 * q : 32 * q + 4, :], scale_rows[32 + 16 * q : 48 + 16 * q : 4, :])
         picked_scales = scale_plane[:].bitcast(U8)[:, 0:S]
         w4_plane = scale_plane[:].bitcast(U8)[:, S:]
 

@@ -1,7 +1,6 @@
 from contextlib import ExitStack
 
 import concourse.mybir as mybir
-from concourse.masks import make_identity
 
 K, M, T, S = 512, 256, 4096, 1536
 FLOPS = 2 * 2 * K * M * S
@@ -54,16 +53,10 @@ def tile_list_tabres_gelu_kernel(
         nc.vector.memset(table_scales[:], 0)
         nc.sync.dma_start(table_scales[32:96:4, :], tab_scales[0].bitcast(I32))
 
-        bias_rows = keep.tile([P, P], F32, name="bias_rows", align_bytes=256)
+        bias_rows = keep.tile([P, 32], F32, name="bias_rows", align_bytes=256)
         nc.vector.memset(bias_rows[:], 0.0)
-        nc.scalar.dma_start(bias_rows[0:HALVES, :], b.rearrange("(h p) -> h p", p=P))
-        identity = keep.tile([P, P], F32, name="identity")
-        nc.vector.memset(identity[:], 0.0)
-        make_identity(nc, identity[:], nomemset=True)
-        bias_turned = psum.tile([P, P], F32, name="bias_turned")
-        nc.tensor.transpose(bias_turned[:], bias_rows[:], identity[:])
-        bias = keep.tile([P, HALVES], F32, name="bias")
-        nc.scalar.copy(bias[:], bias_turned[:, 0:HALVES])
+        for h in range(HALVES):
+            nc.scalar.dma_start(bias_rows[h:P:32, :], b[h * P : (h + 1) * P].rearrange("(q j) -> q j", j=32))
 
         scale_plane = keep.tile([P, (S + M) // 4], I32, name="scale_plane", align_bytes=256)
         nc.vector.memset(scale_plane[:], 0)
@@ -91,7 +84,7 @@ def tile_list_tabres_gelu_kernel(
 
         grouped = []
         for g in range(BANKS):
-            tile = keep.tile([P, PACK * BANK], BF16, name="c_grouped%d" % g, align_bytes=256)
+            tile = keep.tile([P, PACK * BANK], BF16, name="c_grouped%d" % g, tag="c_grouped%d" % g, align_bytes=256)
             split = SCALAR_COLUMNS[g]
             if split > 0:
                 interleave(nc.scalar.copy, tile[:, 0 : PACK * split], c_raw[g][:, :, 0:split])
@@ -121,6 +114,9 @@ def tile_list_tabres_gelu_kernel(
                     start=True,
                     stop=False,
                 )
+
+        bias = keep.tile([P, 32], F32, name="bias", tag="c_grouped%d" % (BANKS - 1), align_bytes=256)
+        nc.vector.transpose(bias[:], bias_rows[:])
 
         for g in range(BANKS):
             cols = slice(g * BANK, (g + 1) * BANK)

@@ -41,9 +41,9 @@ def tile_list_tabres_gelu_kernel(
         psum = ctx.enter_context(tc.psum_pool(name="psum", bufs=1))
 
         offsets = keep.tile([P, S // 16], U16, name="offsets")
-        nc.sync.dma_start(offsets[:], offs)
         u_raw = keep.tile([P, PACK, M], F32, name="u_raw", align_bytes=256)
         nc.sync.dma_start(u_raw[:], u.rearrange("(p t) n -> p t n", t=PACK))
+        nc.sync.dma_start(offsets[:], offs)
 
         scale_rows = keep.tile([P, (S + M) // 4], I32, name="scale_rows", align_bytes=256)
         nc.sync.dma_start(scale_rows[32:96:4, S // 4 :], w4_scales[0].bitcast(I32))
@@ -134,10 +134,13 @@ def tile_list_tabres_gelu_kernel(
                     stop=True,
                 )
 
+        gelu = [keep.tile([P, S], F32, name="activated%d" % h) for h in range(HALVES)]
+        for g in range(BANKS):
+            for h in reversed(range(HALVES)) if g == BANKS - 1 else range(HALVES):
+                nc.scalar.activation(gelu[h][:, g * BANK : (g + 1) * BANK], sums[g, h][:], GELU, bias=bias[:, h : h + 1])
+
         for h in range(HALVES):
-            activated = keep.tile([P, S], F32, name="activated%d" % h)
-            for g in range(BANKS):
-                nc.scalar.activation(activated[:, g * BANK : (g + 1) * BANK], sums[g, h][:], GELU, bias=bias[:, h : h + 1])
+            activated = gelu[h]
             first = 0
             for i, width in enumerate(SLICES[h]):
                 cols = slice(first, first + width)

@@ -22,7 +22,7 @@ HALVES = M // P
 BANK = 512
 BANKS = S // BANK
 SCALAR_COLUMNS = (0, 128, 512)
-SLICES = ((512, 512, 512), (640, 512, 256, 128))
+SLICES = ((512, 512, 512), (736, 416, 256, 128))
 
 
 def interleave(copy, grouped, raw):

@@ -21,7 +21,7 @@ PACK = 4
 HALVES = M // P
 BANK = 512
 BANKS = S // BANK
-SCALAR_COLUMNS = (0, 128, 512)
+SCALAR_COLUMNS = (0, 256, 512)
 SLICES = ((512, 512, 512), (736, 416, 256, 128))
 
 

from contextlib import ExitStack

import concourse.mybir as mybir

K, M, T, S = 512, 256, 4096, 1536
FLOPS = 2 * 2 * K * M * S

F32 = mybir.dt.float32
BF16 = mybir.dt.bfloat16
I32 = mybir.dt.int32
U32 = mybir.dt.uint32
U16 = mybir.dt.uint16
U8 = mybir.dt.uint8
FP8X4 = mybir.dt.float8_e4m3fn_x4
FP4X4 = mybir.dt.float4_e2m1fn_x4
GELU = mybir.ActivationFunctionType.Gelu_apprx_tanh
ADD = mybir.AluOpType.add

P = 128
PACK = 4
HALVES = M // P
BANK = 512
BANKS = S // BANK
SCALAR_COLUMNS = (0, 256, 512)
SLICES = ((512, 512, 512), (736, 416, 256, 128))


def interleave(copy, grouped, raw):
    copy(
        grouped.rearrange("p (c i t) -> p c t i", i=2, t=PACK),
        raw.rearrange("p t (c i) -> p c t i", i=2),
    )


def tile_list_tabres_gelu_kernel(
    tc, tab_words, tab_scales, w4_words, w4_scales, c, u, rT, b, offs, out
):
    nc = tc.nc
    with ExitStack() as ctx:
        keep = ctx.enter_context(tc.tile_pool(name="keep", bufs=1))
        psum = ctx.enter_context(tc.psum_pool(name="psum", bufs=1))

        offsets = keep.tile([P, S // 16], U16, name="offsets")
        u_raw = keep.tile([P, PACK, M], F32, name="u_raw", align_bytes=256)
        nc.sync.dma_start(u_raw[:], u.rearrange("(p t) n -> p t n", t=PACK))
        nc.sync.dma_start(offsets[:], offs)

        scale_rows = keep.tile([P, (S + M) // 4], I32, name="scale_rows", align_bytes=256)
        nc.sync.dma_start(scale_rows[32:96:4, S // 4 :], w4_scales[0].bitcast(I32))
        w4_codes = keep.tile([P, 2 * M], U8, name="w4_codes", align_bytes=256)
        nc.sync.dma_start(w4_codes[:].bitcast(I32), w4_words[0].bitcast(I32))
        table_scales = keep.tile([P, T // 4], I32, name="table_scales", tag="scales_then_u", align_bytes=256)
        nc.vector.memset(table_scales[:], 0)
        nc.sync.dma_start(table_scales[32:96:4, :], tab_scales[0].bitcast(I32))

        bias_rows = keep.tile([P, 32], F32, name="bias_rows", align_bytes=256)
        nc.vector.memset(bias_rows[:], 0.0)
        for h in range(HALVES):
            nc.scalar.dma_start(bias_rows[h:P:32, :], b[h * P : (h + 1) * P].rearrange("(q j) -> q j", j=32))

        scale_plane = keep.tile([P, (S + M) // 4], I32, name="scale_plane", align_bytes=256)
        nc.vector.memset(scale_plane[:], 0)

        c_whole = keep.tile([P, PACK, S], F32, name="c_whole", tag="c_then_residual", align_bytes=256)
        nc.sync.dma_start(c_whole[:], c.rearrange("(p t) j -> p t j", t=PACK))
        c_raw = [c_whole[:, :, g * BANK : (g + 1) * BANK] for g in range(BANKS)]

        table_words = keep.tile([P, T], I32, name="table_words", align_bytes=256)
        nc.sync.dma_start(table_words[:], tab_words[0].rearrange("p t i -> p (t i)").bitcast(I32))

        picked_rows = keep.tile([P, S], U8, name="picked_rows", tag="rows_then_residual", align_bytes=256)
        nc.vector.tensor_copy(picked_rows[:], table_scales[:].bitcast(U8).indirect(offsets[:]))
        nc.vector.tensor_copy(scale_rows[:, 0 : S // 4], picked_rows[:].bitcast(I32))
        for q in range(4):
            nc.sync.dma_start(scale_plane[32 * q : 32 * q + 4, :], scale_rows[32 + 16 * q : 48 + 16 * q : 4, :])
        picked_scales = scale_plane[:].bitcast(U8)[:, 0:S]
        w4_plane = scale_plane[:].bitcast(U8)[:, S:]

        u_grouped = keep.tile([P, PACK * M], BF16, name="u_grouped", tag="scales_then_u", align_bytes=256)
        interleave(nc.scalar.copy, u_grouped[:], u_raw[:])
        u_codes = keep.tile([P, M], U32, name="u_codes", align_bytes=256)
        u_plane = keep.tile([P, M], U8, name="u_plane", align_bytes=256)
        nc.vector.quantize_mx(out=u_codes[:].bitcast(FP8X4), scales=u_plane[:], in_=u_grouped[:])

        grouped = []
        for g in range(BANKS):
            tile = keep.tile([P, PACK * BANK], BF16, name="c_grouped%d" % g, tag="c_grouped%d" % g, align_bytes=256)
            split = SCALAR_COLUMNS[g]
            if split > 0:
                interleave(nc.scalar.copy, tile[:, 0 : PACK * split], c_raw[g][:, :, 0:split])
            if split < BANK:
                interleave(nc.vector.tensor_copy, tile[:, PACK * split :], c_raw[g][:, :, split:])
            grouped.append(tile)

        residual = []
        for h, tag in enumerate(("rows_then_residual", "c_then_residual")):
            window = keep.tile([P, T], F32, name="residual%d" % h, tag=tag, align_bytes=256)
            nc.sync.dma_start(window[:], rT[h * P : (h + 1) * P, :])
            residual.append(window)

        sums = {}
        for g in range(BANKS):
            codes = keep.tile([P, BANK], U32, name="c_codes%d" % g, align_bytes=256)
            plane = keep.tile([P, BANK], U8, name="c_plane%d" % g, align_bytes=256)
            nc.vector.quantize_mx(out=codes[:].bitcast(FP8X4), scales=plane[:], in_=grouped[g][:])
            for h in range(HALVES):
                sums[g, h] = psum.tile([P, BANK], F32, name="sum%d_%d" % (g, h))
                nc.tensor.matmul_mx(
                    out=sums[g, h][:],
                    lhsT=u_codes[:, h * P : (h + 1) * P].bitcast(FP8X4),
                    lhsT_scale=u_plane[:, h * P : (h + 1) * P],
                    rhs=codes[:].bitcast(FP8X4),
                    rhs_scale=plane[:],
                    start=True,
                    stop=False,
                )

        bias = keep.tile([P, 32], F32, name="bias", tag="c_grouped%d" % (BANKS - 1), align_bytes=256)
        nc.vector.transpose(bias[:], bias_rows[:])

        for g in range(BANKS):
            cols = slice(g * BANK, (g + 1) * BANK)
            picked_words = keep.tile([P, BANK], U32, name="picked_words%d" % g, align_bytes=256)
            listed = offsets[:, g * BANK // 16 : (g + 1) * BANK // 16]
            nc.vector.tensor_copy(picked_words[:], table_words[:].bitcast(U32).indirect(listed))
            for h in range(HALVES):
                nc.tensor.matmul_mx(
                    out=sums[g, h][:],
                    lhsT=w4_codes[:, 2 * h * P : 2 * (h + 1) * P].bitcast(FP4X4),
                    lhsT_scale=w4_plane[:, h * P : (h + 1) * P],
                    rhs=picked_words[:].bitcast(FP8X4),
                    rhs_scale=picked_scales[:, cols],
                    start=False,
                    stop=True,
                )

        gelu = [keep.tile([P, S], F32, name="activated%d" % h) for h in range(HALVES)]
        for g in range(BANKS):
            for h in reversed(range(HALVES)) if g == BANKS - 1 else range(HALVES):
                nc.scalar.activation(gelu[h][:, g * BANK : (g + 1) * BANK], sums[g, h][:], GELU, bias=bias[:, h : h + 1])

        for h in range(HALVES):
            activated = gelu[h]
            first = 0
            for i, width in enumerate(SLICES[h]):
                cols = slice(first, first + width)
                result = keep.tile([P, width], F32, name="result%d_%d" % (h, i), align_bytes=256)
                picked = residual[h][:].indirect(offsets[:, first // 16 : (first + width) // 16])
                nc.vector.tensor_tensor(result[:], picked, activated[:, cols], ADD)
                nc.sync.dma_start(out[h * P : (h + 1) * P, cols], result[:])
                first = first + width
